import numpy as np
import ml_dtypes


def mxq(x, axis, fmt="e4m3"):
    dtype, down = {"e4m3": (ml_dtypes.float8_e4m3fn, 7), "e5m2": (ml_dtypes.float8_e5m2, 14)}[fmt]
    v = np.moveaxis(np.asarray(x, np.float32).astype(ml_dtypes.bfloat16).astype(np.float64), axis, -1)
    blocks = v.reshape(v.shape[:-1] + (-1, 32))
    amax = np.abs(blocks).max(-1, keepdims=True)
    byte = np.maximum(np.where(amax > 0, np.frexp(amax)[1] - 1 + 127, 0) - down, 1)
    scale = np.exp2(byte - 127.0)
    codes = (blocks / scale).astype(np.float32).astype(dtype).astype(np.float64)
    return np.moveaxis((codes * scale).reshape(v.shape), -1, axis)


WIDE = False


def mx_kscale(k):
    if not WIDE:
        return np.ones(k)
    levels = np.array([10, -10, 5, -5, 0])
    if k % 512:
        return np.exp2(np.random.permutation(np.resize(levels, k // 32))).repeat(32)
    a = np.empty((k // 512, 16))
    for p in range(k // 512):
        a[p, :8] = np.random.permutation(np.resize(levels, 8))
        for g in range(8):
            far = levels[np.abs(levels - a[p, g]) >= 10]
            a[p, g + 8] = far[np.random.randint(len(far))]
    return np.exp2(a.ravel()).repeat(32)


def f64(x):
    return np.asarray(x).astype(np.float64)


def striped(idx):
    return np.tile(np.asarray(idx).reshape(-1, 16).T, (8, 1)).astype(np.uint16)


def unstriped(offs):
    return offs[:16].T.reshape(-1).astype(np.int64)


def striped8(idx):
    return np.asarray(idx).reshape(8, -1, 16).transpose(0, 2, 1).reshape(128, -1).astype(np.uint16)


def unstriped8(offs):
    return offs.reshape(8, 16, -1).transpose(0, 2, 1).reshape(8, -1).astype(np.int64)


def pick8(x, idx, run):
    r = np.arange(len(x))
    return x[r[:, None], idx[r % (8 * run) // run]]


E2M1 = np.array([0.0, 0.5, 1.0, 1.5, 2.0, 3.0, 4.0, 6.0, -0.0, -0.5, -1.0, -1.5, -2.0, -3.0, -4.0, -6.0])


def pack_weight(w, fmt):
    k, n = w.shape
    w = f64(np.asarray(w, np.float32).astype(ml_dtypes.bfloat16)).reshape(k // 32, 32, n)
    amax = np.abs(w).max(1)
    if fmt == "e4m3":
        byte = np.frexp(amax)[1] - 1 + 127 - 7
    else:
        mant, ex = np.frexp(amax / 6.0)
        byte = np.where(mant > 0.5, ex, ex - 1) + 127
    byte = np.clip(np.where(amax > 0, byte, 1), 1, 254)
    scaled = (w * np.exp2(127.0 - byte)[:, None, :]).reshape(k, n).astype(np.float32)
    by_word = np.ascontiguousarray(scaled.reshape(k // 512, 128, 4, n).transpose(0, 1, 3, 2))
    if fmt == "e4m3":
        words = by_word.astype(ml_dtypes.float8_e4m3fn).view(np.uint8)
    else:
        c = by_word.astype(ml_dtypes.float4_e2m1fn).view(np.uint8) & 0xF
        words = (c[..., 0::2] | (c[..., 1::2] << 4)).reshape(k // 512, 128, 2 * n)
    return np.ascontiguousarray(words), np.ascontiguousarray(byte.astype(np.uint8).reshape(k // 512, 16, n))


def unpack_weight(words, scales, fmt):
    g, _, n = scales.shape
    words = np.ascontiguousarray(words).reshape(g, 128, n, -1)
    if fmt == "e4m3":
        vals = words.view(ml_dtypes.float8_e4m3fn).astype(np.float64)
    else:
        nib = np.empty((g, 128, n, 4), np.uint8)
        nib[..., 0::2] = words & 0xF
        nib[..., 1::2] = words >> 4
        vals = E2M1[nib]
    vals = vals * np.repeat(np.exp2(scales.astype(np.float64) - 127.0), 8, axis=1)[..., None]
    return vals.transpose(0, 1, 3, 2).reshape(g * 512, n)


def sgn(shape):
    return np.random.uniform(0.5, 2.0, shape) * np.where(np.random.standard_normal(shape) < 0, -1.0, 1.0)


K, J, R, T, F, O, N, U, E = 512, 1024, 512, 2048, 1024, 512, 256, 256, 1024


def setup_inputs():
    n = np.random.standard_normal
    idx = np.random.permutation(T)[:J]
    idx2 = np.stack([np.random.permutation(F)[:R] for _ in range(8)])
    idx3 = np.stack([np.random.permutation(F)[:R] for _ in range(8)])
    idx4 = np.random.permutation(J)[:O]
    idx5 = np.stack([np.random.permutation(J)[:O] for _ in range(8)])
    idx6 = np.stack([np.random.permutation(O)[:U] for _ in range(8)])
    idx7 = np.stack([np.random.permutation(E)[:U] for _ in range(8)])
    fk = mx_kscale(K)
    fr = mx_kscale(R)
    xtp = pack_weight(n((K, T)) * fk[:, None], "e2m1")
    wbp = pack_weight(n((R, N)) * 1 / np.sqrt(R) / fr[:, None], "e2m1")
    return {
        "xt_words": xtp[0],
        "xt_scales": xtp[1],
        "ua": (np.random.randint(-7, 8, (K, F)).astype(np.float64)).astype(np.float32),
        "ha": ((np.random.randint(10, 25, (K, 1)) / 1024.0) / fk[:, None]).astype(np.float32),
        "hb": ((np.random.randint(4, 13, (K, 1)) / 1024.0) / fk[:, None]).astype(np.float32),
        "sa": (np.random.uniform(0.5, 1.6, (R, 1)) * fr[:, None]).astype(np.float32),
        "sb": (np.random.uniform(0.5, 1.6, (R, 1)) * fr[:, None]).astype(np.float32),
        "wb_words": wbp[0],
        "wb_scales": wbp[1],
        "so": (sgn((N, 1))).astype(np.float32),
        "offs": striped(idx),
        "offs2": striped8(idx2),
        "offs3": striped8(idx3),
        "offs4": striped(idx4),
        "offs5": striped8(idx5),
        "offs6": striped8(idx6),
        "offs7": striped8(idx7),
    }


def reference(xt_words, xt_scales, ua, ha, hb, sa, sb, wb_words, wb_scales, so, offs, offs2, offs3, offs4, offs5, offs6, offs7):
    idx = unstriped(offs)
    idx2 = unstriped8(offs2)
    idx3 = unstriped8(offs3)
    idx4 = unstriped(offs4)
    idx5 = unstriped8(offs5)
    idx6 = unstriped8(offs6)
    idx7 = unstriped8(offs7)
    xtu = unpack_weight(xt_words, xt_scales, "e2m1")
    wbu = unpack_weight(wb_words, wb_scales, "e2m1")
    wc = pick8(f64(ua), idx2, 64) * f64(ha) + pick8(f64(ua), idx3, 64) * f64(hb)
    wcq = mxq(wc, 0, "e4m3")
    xtidxg = xtu[:, idx]
    a = wcq.T @ xtidxg
    hid = np.maximum(a[:, idx4] * f64(sa), pick8(a, idx5, 64) * f64(sb))
    hidq = mxq(hid, 0, "e4m3")
    p = wbu.T @ hidq
    m0 = pick8(p, idx6, 16) * f64(so)
    y = np.zeros((N, E))
    y[np.arange(N)[:, None], idx7[np.arange(N) % 128 // 16]] = m0
    return y

@@ -1,0 +1,216 @@
+from contextlib import ExitStack
+
+import concourse.mybir as mybir
+
+K, J, R, T, F, O, N, U, E = 512, 1024, 512, 2048, 1024, 512, 256, 256, 1024
+FLOPS = 2 * K * R * J + 2 * R * N * O
+
+F32 = mybir.dt.float32
+BF16 = mybir.dt.bfloat16
+I32 = mybir.dt.int32
+U32 = mybir.dt.uint32
+U16 = mybir.dt.uint16
+U8 = mybir.dt.uint8
+FP8X4 = mybir.dt.float8_e4m3fn_x4
+FP4X4 = mybir.dt.float4_e2m1fn_x4
+COPY = mybir.ActivationFunctionType.Copy
+ADD = mybir.AluOpType.add
+MAX = mybir.AluOpType.max
+
+P = 128
+PACK = 4
+BANK = 512
+
+
+def tile_picked_tokens_refined_one_mixedpair_one_posted_kernel(
+    tc, xt_words, xt_scales, ua, ha, hb, sa, sb, wb_words, wb_scales, so,
+    offs, offs2, offs3, offs4, offs5, offs6, offs7, out,
+):
+    nc = tc.nc
+    with ExitStack() as ctx:
+        lists = ctx.enter_context(tc.tile_pool(name="lists", bufs=1))
+        keep = ctx.enter_context(tc.tile_pool(name="keep", bufs=1))
+        psum = ctx.enter_context(tc.psum_pool(name="psum", bufs=1))
+
+        def load_list(src, name):
+            tile = lists.tile(list(src.shape), U16, name=name)
+            nc.sync.dma_start(tile[:], src)
+            return tile
+
+        def load_rows4(src, name, queue):
+            tile = keep.tile([P, PACK], F32, name=name)
+            queue.dma_start(tile[:], src.rearrange("(p j) o -> p (j o)", j=PACK))
+            return tile
+
+        def load_scale_rows(tile, src):
+            for q in range(4):
+                nc.sync.dma_start(tile[32 * q : 32 * q + 4, :].bitcast(I32), src[0, 4 * q : 4 * q + 4, :].bitcast(I32))
+
+        def entries(tile, lo, hi):
+            return tile[:, lo // 16 : hi // 16]
+
+        xt_s = keep.tile([P, T], U8, name="xt_s", align_bytes=64)
+        nc.vector.memset(xt_s[:].bitcast(I32), 0)
+        wb_s = keep.tile([P, N], U8, name="wb_s", align_bytes=64)
+        nc.vector.memset(wb_s[:].bitcast(I32), 0)
+        pages = [keep.tile([P, E], F32, name="page%d" % b) for b in range(N // P)]
+        for page in pages:
+            nc.vector.memset(page[:], 0.0)
+
+        ua_rows = ua.rearrange("(p j) f -> j p f", j=PACK)
+        ua_sb = [keep.tile([P, F], F32, name="ua%d" % j) for j in range(PACK)]
+        ha_sb = load_rows4(ha, "ha_sb", nc.scalar)
+        hb_sb = load_rows4(hb, "hb_sb", nc.scalar)
+        list2 = load_list(offs2, "list2")
+        nc.sync.dma_start(ua_sb[0][:], ua_rows[0])
+        list3 = load_list(offs3, "list3")
+        list1 = load_list(offs, "list1")
+        xt_w = keep.tile([P, T], U16, name="xt_w", align_bytes=64)
+        nc.sync.dma_start(xt_w[:].bitcast(I32), xt_words[0].bitcast(I32))
+        nc.sync.dma_start(ua_sb[1][:], ua_rows[1])
+        load_scale_rows(xt_s, xt_scales)
+        nc.sync.dma_start(ua_sb[2][:], ua_rows[2])
+        nc.sync.dma_start(ua_sb[3][:], ua_rows[3])
+        list5 = load_list(offs5, "list5")
+        sb_sb = load_rows4(sb, "sb_sb", nc.sync)
+        list4 = load_list(offs4, "list4")
+        sa_sb = load_rows4(sa, "sa_sb", nc.sync)
+        wb_w = keep.tile([P, 2 * N], U8, name="wb_w", align_bytes=64)
+        nc.sync.dma_start(wb_w[:].bitcast(I32), wb_words[0].bitcast(I32))
+        load_scale_rows(wb_s, wb_scales)
+        list6 = load_list(offs6, "list6")
+        list7 = load_list(offs7, "list7")
+        so_sb = [keep.tile([P, 1], F32, name="so%d" % b) for b in range(N // P)]
+        for b in range(N // P):
+            nc.sync.dma_start(so_sb[b][:], so[b * P : (b + 1) * P, :])
+
+        xg_w = keep.tile([P, J], U16, name="xg_w", align_bytes=64)
+        xg_s = keep.tile([P, J], U8, name="xg_s", align_bytes=64)
+        for lo in range(0, J, BANK):
+            nc.vector.tensor_copy(xg_w[:, lo : lo + BANK], xt_w[:].indirect(entries(list1, lo, lo + BANK)))
+            nc.vector.tensor_copy(xg_s[:, lo : lo + BANK], xt_s[:].indirect(entries(list1, lo, lo + BANK)))
+
+        g2 = keep.tile([P, PACK, R], F32, name="g2")
+        g3 = keep.tile([P, PACK, R], F32, name="g3")
+
+        def fetch_wc(j, lo, hi):
+            nc.scalar.activation(g2[:, j, lo:hi], ua_sb[j][:].indirect(entries(list2, lo, hi)), COPY, scale=ha_sb[:, j : j + 1])
+            nc.scalar.activation(g3[:, j, lo:hi], ua_sb[j][:].indirect(entries(list3, lo, hi)), COPY, scale=hb_sb[:, j : j + 1])
+
+        wc_in = keep.tile([P, PACK, P, PACK], BF16, name="wc_in", align_bytes=64)
+        wc_w = keep.tile([P, R], U32, name="wc_w", align_bytes=64)
+        wc_s = keep.tile([P, R], U8, name="wc_s", align_bytes=64)
+
+        def add_wc(half, pair):
+            ms = slice(64 * half, 64 * (half + 1))
+            ts = slice(2 * pair, 2 * pair + 2)
+            nc.vector.tensor_tensor(
+                wc_in[:, ts, ms, :].rearrange("p t m j -> p m j t"),
+                g2[:].rearrange("p j (m t) -> p m j t", t=PACK)[:, ms, :, ts],
+                g3[:].rearrange("p j (m t) -> p m j t", t=PACK)[:, ms, :, ts],
+                ADD,
+            )
+
+        def add_wc_part(ts, js):
+            ms = slice(64, 128)
+            nc.vector.tensor_tensor(
+                wc_in[:, ts, ms, js].rearrange("p t m j -> p m j t"),
+                g2[:].rearrange("p j (m t) -> p m j t", t=PACK)[:, ms, js, ts],
+                g3[:].rearrange("p j (m t) -> p m j t", t=PACK)[:, ms, js, ts],
+                ADD,
+            )
+
+        def quantize_wc(t):
+            cols = slice(P * t, P * (t + 1))
+            nc.vector.quantize_mx(wc_w[:, cols].bitcast(FP8X4), wc_s[:, cols], wc_in[:, t].rearrange("p m j -> p (m j)"))
+
+        half_r = R // 2
+        fetch_wc(0, 0, R)
+        fetch_wc(1, 0, R)
+        fetch_wc(2, 0, half_r)
+        fetch_wc(3, 0, half_r)
+        add_wc(0, 0)
+        add_wc(0, 1)
+        fetch_wc(2, half_r, R)
+        add_wc_part(slice(0, PACK), slice(0, 3))
+        fetch_wc(3, half_r, R)
+
+        a_sb = [keep.tile([P, J], F32, name="a%d" % t) for t in range(PACK)]
+        banks = [psum.tile([P, BANK], F32, name="bank%d" % i) for i in range(8)]
+
+        def first_product(t, lo, hi, acc):
+            cols = slice(P * t, P * (t + 1))
+            nc.tensor.matmul_mx(acc, lhsT=wc_w[:, cols].bitcast(FP8X4), lhsT_scale=wc_s[:, cols],
+                                rhs=xg_w[:, lo:hi].bitcast(FP4X4), rhs_scale=xg_s[:, lo:hi], start=True, stop=True)
+
+        add_wc_part(slice(0, 1), slice(3, PACK))
+        add_wc_part(slice(1, 2), slice(3, PACK))
+        quantize_wc(0)
+        add_wc_part(slice(2, PACK), slice(3, PACK))
+        for t in range(1, PACK):
+            quantize_wc(t)
+        first_product(0, 0, 512, banks[0][:])
+        nc.scalar.copy(a_sb[0][:, :512], banks[0][:])
+        first_product(0, 512, 768, banks[1][:, :256])
+        nc.vector.tensor_copy(a_sb[0][:, 512:768], banks[1][:, :256])
+        first_product(0, 768, J, banks[2][:, :256])
+        nc.vector.tensor_copy(a_sb[0][:, 768:], banks[2][:, :256])
+        for t in range(1, PACK):
+            for h in range(2):
+                bank = banks[(2 * t + h + 1) % 8]
+                first_product(t, BANK * h, BANK * (h + 1), bank[:])
+                nc.vector.tensor_copy(a_sb[t][:, BANK * h : BANK * (h + 1)], bank[:])
+
+        g4 = keep.tile([P, PACK, O], F32, name="g4")
+        g5 = keep.tile([P, PACK, O], F32, name="g5")
+
+        def fetch4(t, lo, hi):
+            nc.scalar.activation(g4[:, t, lo:hi], a_sb[t][:].indirect(entries(list4, lo, hi)), COPY, scale=sa_sb[:, t : t + 1])
+
+        def fetch5(t, lo, hi):
+            nc.scalar.activation(g5[:, t, lo:hi], a_sb[t][:].indirect(entries(list5, lo, hi)), COPY, scale=sb_sb[:, t : t + 1])
+
+        hid_in = keep.tile([P, O, PACK], BF16, name="hid_in", align_bytes=64)
+        hid_w = keep.tile([P, O], U32, name="hid_w", align_bytes=64)
+        hid_s = keep.tile([P, O], U8, name="hid_s", align_bytes=64)
+        p_sb = [keep.tile([P, O], F32, name="p%d" % b) for b in range(N // P)]
+
+        def hidden(lo, hi):
+            nc.vector.tensor_tensor(
+                hid_in[:, lo:hi, :].rearrange("p (c i) t -> p c t i", i=2),
+                g4[:, :, lo:hi].rearrange("p t (c i) -> p c t i", i=2),
+                g5[:, :, lo:hi].rearrange("p t (c i) -> p c t i", i=2),
+                MAX,
+            )
+            nc.vector.quantize_mx(hid_w[:, lo:hi].bitcast(FP8X4), hid_s[:, lo:hi], hid_in[:, lo:hi, :].rearrange("p o t -> p (o t)"))
+
+        def second_product(lo, hi, first_bank, copies_out):
+            for b in range(N // P):
+                acc = banks[first_bank + b][:, : hi - lo]
+                nc.tensor.matmul_mx(acc, lhsT=wb_w[:, 2 * P * b : 2 * P * (b + 1)].bitcast(FP4X4), lhsT_scale=wb_s[:, P * b : P * (b + 1)],
+                                    rhs=hid_w[:, lo:hi].bitcast(FP8X4), rhs_scale=hid_s[:, lo:hi], start=True, stop=True)
+                copies_out[b](p_sb[b][:, lo:hi], acc)
+
+        for t in range(2):
+            fetch5(t, 0, O)
+            fetch4(t, 0, O)
+        for t in range(2, PACK):
+            fetch5(t, 0, 256)
+            fetch4(t, 0, 256)
+        hidden(0, 256)
+        for t in range(2, PACK):
+            fetch5(t, 256, O)
+        for lo in range(256, O, 128):
+            for t in range(2, PACK):
+                fetch4(t, lo, lo + 128)
+            hidden(lo, lo + 128)
+        second_product(0, 256, 1, [nc.scalar.copy, nc.scalar.copy])
+        second_product(256, 384, 3, [nc.scalar.copy, nc.scalar.copy])
+        second_product(384, O, 5, [nc.scalar.copy, nc.vector.tensor_copy])
+
+        m0 = keep.tile([P, N // P, U], F32, name="m0")
+        for b, lo, hi in ((0, 0, U // 2), (1, 0, U), (0, U // 2, U)):
+            nc.scalar.activation(m0[:, b, lo:hi], p_sb[b][:].indirect(entries(list6, lo, hi)), COPY, scale=so_sb[b][:])
+            nc.vector.tensor_copy(pages[b][:].indirect(entries(list7, lo, hi)), m0[:, b, lo:hi])
+            if hi == U:
+                nc.sync.dma_start(out[b * P : (b + 1) * P, :], pages[b][:])

@@ -61,6 +61,9 @@ def tile_picked_tokens_refined_one_mixedpair_one_posted_kernel(
         ua_sb = [keep.tile([P, F], F32, name="ua%d" % j) for j in range(PACK)]
         ha_sb = load_rows4(ha, "ha_sb", nc.scalar)
         hb_sb = load_rows4(hb, "hb_sb", nc.scalar)
+        warm = keep.tile([P, 2, 8], F32, name="warm")
+        nc.gpsimd.memset(warm[:, 0, :], 0.0)
+        nc.scalar.activation(warm[:, 1, :], warm[:, 0, :], COPY)
         list2 = load_list(offs2, "list2")
         nc.sync.dma_start(ua_sb[0][:], ua_rows[0])
         list3 = load_list(offs3, "list3")

@@ -64,8 +64,8 @@ def tile_picked_tokens_refined_one_mixedpair_one_posted_kernel(
         warm = keep.tile([P, 2, 8], F32, name="warm")
         nc.gpsimd.memset(warm[:, 0, :], 0.0)
         nc.scalar.activation(warm[:, 1, :], warm[:, 0, :], COPY)
-        list2 = load_list(offs2, "list2")
         nc.sync.dma_start(ua_sb[0][:], ua_rows[0])
+        list2 = load_list(offs2, "list2")
         list3 = load_list(offs3, "list3")
         list1 = load_list(offs, "list1")
         xt_w = keep.tile([P, T], U16, name="xt_w", align_bytes=64)
@@ -104,22 +104,22 @@ def tile_picked_tokens_refined_one_mixedpair_one_posted_kernel(
         wc_w = keep.tile([P, R], U32, name="wc_w", align_bytes=64)
         wc_s = keep.tile([P, R], U8, name="wc_s", align_bytes=64)
 
-        def add_wc(half, pair):
-            ms = slice(64 * half, 64 * (half + 1))
-            ts = slice(2 * pair, 2 * pair + 2)
-            nc.vector.tensor_tensor(
-                wc_in[:, ts, ms, :].rearrange("p t m j -> p m j t"),
-                g2[:].rearrange("p j (m t) -> p m j t", t=PACK)[:, ms, :, ts],
-                g3[:].rearrange("p j (m t) -> p m j t", t=PACK)[:, ms, :, ts],
-                ADD,
+        wc_sum = keep.tile([P, PACK, R], BF16, name="wc_sum")
+
+        def add_wc(j, lo, hi):
+            nc.vector.tensor_tensor(wc_sum[:, j, lo:hi], g2[:, j, lo:hi], g3[:, j, lo:hi], ADD)
+
+        def deal_wc(half, planes):
+            nc.vector.tensor_copy(
+                wc_in[:].rearrange("p t (h c i) j -> p h c t i j", h=2, i=2)[:, half, :, :, :, :planes],
+                wc_sum[:].rearrange("p j (h c i t) -> p h c t i j", h=2, i=2, t=PACK)[:, half, :, :, :, :planes],
             )
 
-        def add_wc_part(ts, js):
-            ms = slice(64, 128)
+        def add_last_wc(ts):
             nc.vector.tensor_tensor(
-                wc_in[:, ts, ms, js].rearrange("p t m j -> p m j t"),
-                g2[:].rearrange("p j (m t) -> p m j t", t=PACK)[:, ms, js, ts],
-                g3[:].rearrange("p j (m t) -> p m j t", t=PACK)[:, ms, js, ts],
+                wc_in[:, ts, 64:, PACK - 1].rearrange("p t m -> p m t"),
+                g2[:, PACK - 1, R // 2 :].rearrange("p (m t) -> p m t", t=PACK)[:, :, ts],
+                g3[:, PACK - 1, R // 2 :].rearrange("p (m t) -> p m t", t=PACK)[:, :, ts],
                 ADD,
             )
 
@@ -128,17 +128,16 @@ def tile_picked_tokens_refined_one_mixedpair_one_posted_kernel(
             nc.vector.quantize_mx(wc_w[:, cols].bitcast(FP8X4), wc_s[:, cols], wc_in[:, t].rearrange("p m j -> p (m j)"))
 
         half_r = R // 2
-        fetch_wc(0, 0, R)
-        fetch_wc(1, 0, R)
-        fetch_wc(2, 0, half_r)
-        fetch_wc(3, 0, half_r)
-        add_wc(0, 0)
-        add_wc(0, 1)
-        fetch_wc(2, half_r, R)
-        add_wc_part(slice(0, PACK), slice(0, 3))
-        fetch_wc(3, half_r, R)
+        for j in range(PACK - 1):
+            fetch_wc(j, 0, R)
+            add_wc(j, 0, R)
+        deal_wc(1, PACK - 1)
+        fetch_wc(PACK - 1, 0, half_r)
+        add_wc(PACK - 1, 0, half_r)
+        deal_wc(0, PACK)
+        fetch_wc(PACK - 1, half_r, R)
 
-        a_sb = [keep.tile([P, J], F32, name="a%d" % t) for t in range(PACK)]
+        a_sb = [keep.tile([P, J], F32, name="a%d" % t, tag="a%d" % t) for t in range(PACK)]
         banks = [psum.tile([P, BANK], F32, name="bank%d" % i) for i in range(8)]
 
         def first_product(t, lo, hi, acc):
@@ -146,10 +145,10 @@ def tile_picked_tokens_refined_one_mixedpair_one_posted_kernel(
             nc.tensor.matmul_mx(acc, lhsT=wc_w[:, cols].bitcast(FP8X4), lhsT_scale=wc_s[:, cols],
                                 rhs=xg_w[:, lo:hi].bitcast(FP4X4), rhs_scale=xg_s[:, lo:hi], start=True, stop=True)
 
-        add_wc_part(slice(0, 1), slice(3, PACK))
-        add_wc_part(slice(1, 2), slice(3, PACK))
+        add_last_wc(slice(0, 1))
+        add_last_wc(slice(1, 2))
         quantize_wc(0)
-        add_wc_part(slice(2, PACK), slice(3, PACK))
+        add_last_wc(slice(2, PACK))
         for t in range(1, PACK):
             quantize_wc(t)
         first_product(0, 0, 512, banks[0][:])
@@ -158,11 +157,14 @@ def tile_picked_tokens_refined_one_mixedpair_one_posted_kernel(
         nc.vector.tensor_copy(a_sb[0][:, 512:768], banks[1][:, :256])
         first_product(0, 768, J, banks[2][:, :256])
         nc.vector.tensor_copy(a_sb[0][:, 768:], banks[2][:, :256])
-        for t in range(1, PACK):
-            for h in range(2):
-                bank = banks[(2 * t + h + 1) % 8]
-                first_product(t, BANK * h, BANK * (h + 1), bank[:])
+        for i, (t, h) in enumerate(((1, 0), (1, 1), (2, 0), (3, 0), (2, 1), (3, 1))):
+            bank = banks[(3 + i) % 8]
+            first_product(t, BANK * h, BANK * (h + 1), bank[:])
+            if i < 4:
                 nc.vector.tensor_copy(a_sb[t][:, BANK * h : BANK * (h + 1)], bank[:])
+        for lo, hi in ((0, 384), (384, 512)):
+            for t, bank in ((2, banks[7]), (3, banks[0])):
+                nc.vector.tensor_copy(a_sb[t][:, BANK + lo : BANK + hi], bank[:, lo:hi])
 
         g4 = keep.tile([P, PACK, O], F32, name="g4")
         g5 = keep.tile([P, PACK, O], F32, name="g5")
@@ -176,15 +178,22 @@ def tile_picked_tokens_refined_one_mixedpair_one_posted_kernel(
         hid_in = keep.tile([P, O, PACK], BF16, name="hid_in", align_bytes=64)
         hid_w = keep.tile([P, O], U32, name="hid_w", align_bytes=64)
         hid_s = keep.tile([P, O], U8, name="hid_s", align_bytes=64)
-        p_sb = [keep.tile([P, O], F32, name="p%d" % b) for b in range(N // P)]
 
-        def hidden(lo, hi):
-            nc.vector.tensor_tensor(
-                hid_in[:, lo:hi, :].rearrange("p (c i) t -> p c t i", i=2),
-                g4[:, :, lo:hi].rearrange("p t (c i) -> p c t i", i=2),
-                g5[:, :, lo:hi].rearrange("p t (c i) -> p c t i", i=2),
-                MAX,
+        half_o = O // 2
+        hid = keep.tile([P, PACK, half_o], BF16, name="hid")
+
+        def larger(ts, lo, hi):
+            cols = slice(lo % half_o, lo % half_o + hi - lo)
+            nc.vector.tensor_tensor(hid[:, ts, cols], g4[:, ts, lo:hi], g5[:, ts, lo:hi], MAX)
+
+        def interleave_hidden(lo, hi):
+            cols = slice(lo % half_o, lo % half_o + hi - lo)
+            nc.vector.tensor_copy(
+                hid_in[:, lo:hi, :].rearrange("p (c i) t -> p c t i", i=4),
+                hid[:, :, cols].rearrange("p t (c i) -> p c t i", i=4),
             )
+
+        def quantize_hidden(lo, hi):
             nc.vector.quantize_mx(hid_w[:, lo:hi].bitcast(FP8X4), hid_s[:, lo:hi], hid_in[:, lo:hi, :].rearrange("p o t -> p (o t)"))
 
         def second_product(lo, hi, first_bank, copies_out):
@@ -197,16 +206,22 @@ def tile_picked_tokens_refined_one_mixedpair_one_posted_kernel(
         for t in range(2):
             fetch5(t, 0, O)
             fetch4(t, 0, O)
+        for t, ts in ((2, slice(0, 3)), (3, slice(3, PACK))):
+            fetch5(t, 0, half_o)
+            fetch4(t, 0, half_o)
+            larger(ts, 0, half_o)
+        interleave_hidden(0, half_o)
+        larger(slice(0, 2), half_o, O)
+        quantize_hidden(0, half_o)
         for t in range(2, PACK):
-            fetch5(t, 0, 256)
-            fetch4(t, 0, 256)
-        hidden(0, 256)
-        for t in range(2, PACK):
-            fetch5(t, 256, O)
-        for lo in range(256, O, 128):
+            fetch5(t, half_o, O)
+        for lo in range(half_o, O, 128):
             for t in range(2, PACK):
                 fetch4(t, lo, lo + 128)
-            hidden(lo, lo + 128)
+                larger(slice(t, t + 1), lo, lo + 128)
+            interleave_hidden(lo, lo + 128)
+            quantize_hidden(lo, lo + 128)
+        p_sb = [keep.tile([P, O], F32, name="p%d" % b, tag="a%d" % (3 - b)) for b in range(N // P)]
         second_product(0, 256, 1, [nc.scalar.copy, nc.scalar.copy])
         second_product(256, 384, 3, [nc.scalar.copy, nc.scalar.copy])
         second_product(384, O, 5, [nc.scalar.copy, nc.vector.tensor_copy])

from contextlib import ExitStack

import concourse.mybir as mybir

K, J, R, T, F, O, N, U, E = 512, 1024, 512, 2048, 1024, 512, 256, 256, 1024
FLOPS = 2 * K * R * J + 2 * R * N * O

F32 = mybir.dt.float32
BF16 = mybir.dt.bfloat16
I32 = mybir.dt.int32
U32 = mybir.dt.uint32
U16 = mybir.dt.uint16
U8 = mybir.dt.uint8
FP8X4 = mybir.dt.float8_e4m3fn_x4
FP4X4 = mybir.dt.float4_e2m1fn_x4
COPY = mybir.ActivationFunctionType.Copy
ADD = mybir.AluOpType.add
MAX = mybir.AluOpType.max

P = 128
PACK = 4
BANK = 512


def tile_picked_tokens_refined_one_mixedpair_one_posted_kernel(
    tc, xt_words, xt_scales, ua, ha, hb, sa, sb, wb_words, wb_scales, so,
    offs, offs2, offs3, offs4, offs5, offs6, offs7, out,
):
    nc = tc.nc
    with ExitStack() as ctx:
        lists = ctx.enter_context(tc.tile_pool(name="lists", bufs=1))
        keep = ctx.enter_context(tc.tile_pool(name="keep", bufs=1))
        psum = ctx.enter_context(tc.psum_pool(name="psum", bufs=1))

        def load_list(src, name):
            tile = lists.tile(list(src.shape), U16, name=name)
            nc.sync.dma_start(tile[:], src)
            return tile

        def load_rows4(src, name, queue):
            tile = keep.tile([P, PACK], F32, name=name)
            queue.dma_start(tile[:], src.rearrange("(p j) o -> p (j o)", j=PACK))
            return tile

        def load_scale_rows(tile, src):
            for q in range(4):
                nc.sync.dma_start(tile[32 * q : 32 * q + 4, :].bitcast(I32), src[0, 4 * q : 4 * q + 4, :].bitcast(I32))

        def entries(tile, lo, hi):
            return tile[:, lo // 16 : hi // 16]

        xt_s = keep.tile([P, T], U8, name="xt_s", align_bytes=64)
        nc.vector.memset(xt_s[:].bitcast(I32), 0)
        wb_s = keep.tile([P, N], U8, name="wb_s", align_bytes=64)
        nc.vector.memset(wb_s[:].bitcast(I32), 0)
        pages = [keep.tile([P, E], F32, name="page%d" % b) for b in range(N // P)]
        for page in pages:
            nc.vector.memset(page[:], 0.0)

        ua_rows = ua.rearrange("(p j) f -> j p f", j=PACK)
        ua_sb = [keep.tile([P, F], F32, name="ua%d" % j) for j in range(PACK)]
        ha_sb = load_rows4(ha, "ha_sb", nc.scalar)
        hb_sb = load_rows4(hb, "hb_sb", nc.scalar)
        warm = keep.tile([P, 2, 8], F32, name="warm")
        nc.gpsimd.memset(warm[:, 0, :], 0.0)
        nc.scalar.activation(warm[:, 1, :], warm[:, 0, :], COPY)
        nc.sync.dma_start(ua_sb[0][:], ua_rows[0])
        list2 = load_list(offs2, "list2")
        list3 = load_list(offs3, "list3")
        list1 = load_list(offs, "list1")
        xt_w = keep.tile([P, T], U16, name="xt_w", align_bytes=64)
        nc.sync.dma_start(xt_w[:].bitcast(I32), xt_words[0].bitcast(I32))
        nc.sync.dma_start(ua_sb[1][:], ua_rows[1])
        load_scale_rows(xt_s, xt_scales)
        nc.sync.dma_start(ua_sb[2][:], ua_rows[2])
        nc.sync.dma_start(ua_sb[3][:], ua_rows[3])
        list5 = load_list(offs5, "list5")
        sb_sb = load_rows4(sb, "sb_sb", nc.sync)
        list4 = load_list(offs4, "list4")
        sa_sb = load_rows4(sa, "sa_sb", nc.sync)
        wb_w = keep.tile([P, 2 * N], U8, name="wb_w", align_bytes=64)
        nc.sync.dma_start(wb_w[:].bitcast(I32), wb_words[0].bitcast(I32))
        load_scale_rows(wb_s, wb_scales)
        list6 = load_list(offs6, "list6")
        list7 = load_list(offs7, "list7")
        so_sb = [keep.tile([P, 1], F32, name="so%d" % b) for b in range(N // P)]
        for b in range(N // P):
            nc.sync.dma_start(so_sb[b][:], so[b * P : (b + 1) * P, :])

        xg_w = keep.tile([P, J], U16, name="xg_w", align_bytes=64)
        xg_s = keep.tile([P, J], U8, name="xg_s", align_bytes=64)
        for lo in range(0, J, BANK):
            nc.vector.tensor_copy(xg_w[:, lo : lo + BANK], xt_w[:].indirect(entries(list1, lo, lo + BANK)))
            nc.vector.tensor_copy(xg_s[:, lo : lo + BANK], xt_s[:].indirect(entries(list1, lo, lo + BANK)))

        g2 = keep.tile([P, PACK, R], F32, name="g2")
        g3 = keep.tile([P, PACK, R], F32, name="g3")

        def fetch_wc(j, lo, hi):
            nc.scalar.activation(g2[:, j, lo:hi], ua_sb[j][:].indirect(entries(list2, lo, hi)), COPY, scale=ha_sb[:, j : j + 1])
            nc.scalar.activation(g3[:, j, lo:hi], ua_sb[j][:].indirect(entries(list3, lo, hi)), COPY, scale=hb_sb[:, j : j + 1])

        wc_in = keep.tile([P, PACK, P, PACK], BF16, name="wc_in", align_bytes=64)
        wc_w = keep.tile([P, R], U32, name="wc_w", align_bytes=64)
        wc_s = keep.tile([P, R], U8, name="wc_s", align_bytes=64)

        wc_sum = keep.tile([P, PACK, R], BF16, name="wc_sum")

        def add_wc(j, lo, hi):
            nc.vector.tensor_tensor(wc_sum[:, j, lo:hi], g2[:, j, lo:hi], g3[:, j, lo:hi], ADD)

        def deal_wc(half, planes):
            nc.vector.tensor_copy(
                wc_in[:].rearrange("p t (h c i) j -> p h c t i j", h=2, i=2)[:, half, :, :, :, :planes],
                wc_sum[:].rearrange("p j (h c i t) -> p h c t i j", h=2, i=2, t=PACK)[:, half, :, :, :, :planes],
            )

        def add_last_wc(ts):
            nc.vector.tensor_tensor(
                wc_in[:, ts, 64:, PACK - 1].rearrange("p t m -> p m t"),
                g2[:, PACK - 1, R // 2 :].rearrange("p (m t) -> p m t", t=PACK)[:, :, ts],
                g3[:, PACK - 1, R // 2 :].rearrange("p (m t) -> p m t", t=PACK)[:, :, ts],
                ADD,
            )

        def quantize_wc(t):
            cols = slice(P * t, P * (t + 1))
            nc.vector.quantize_mx(wc_w[:, cols].bitcast(FP8X4), wc_s[:, cols], wc_in[:, t].rearrange("p m j -> p (m j)"))

        half_r = R // 2
        for j in range(PACK - 1):
            fetch_wc(j, 0, R)
            add_wc(j, 0, R)
        deal_wc(1, PACK - 1)
        fetch_wc(PACK - 1, 0, half_r)
        add_wc(PACK - 1, 0, half_r)
        deal_wc(0, PACK)
        fetch_wc(PACK - 1, half_r, R)

        a_sb = [keep.tile([P, J], F32, name="a%d" % t, tag="a%d" % t) for t in range(PACK)]
        banks = [psum.tile([P, BANK], F32, name="bank%d" % i) for i in range(8)]

        def first_product(t, lo, hi, acc):
            cols = slice(P * t, P * (t + 1))
            nc.tensor.matmul_mx(acc, lhsT=wc_w[:, cols].bitcast(FP8X4), lhsT_scale=wc_s[:, cols],
                                rhs=xg_w[:, lo:hi].bitcast(FP4X4), rhs_scale=xg_s[:, lo:hi], start=True, stop=True)

        add_last_wc(slice(0, 1))
        add_last_wc(slice(1, 2))
        quantize_wc(0)
        add_last_wc(slice(2, PACK))
        for t in range(1, PACK):
            quantize_wc(t)
        first_product(0, 0, 512, banks[0][:])
        nc.scalar.copy(a_sb[0][:, :512], banks[0][:])
        first_product(0, 512, 768, banks[1][:, :256])
        nc.vector.tensor_copy(a_sb[0][:, 512:768], banks[1][:, :256])
        first_product(0, 768, J, banks[2][:, :256])
        nc.vector.tensor_copy(a_sb[0][:, 768:], banks[2][:, :256])
        for i, (t, h) in enumerate(((1, 0), (1, 1), (2, 0), (3, 0), (2, 1), (3, 1))):
            bank = banks[(3 + i) % 8]
            first_product(t, BANK * h, BANK * (h + 1), bank[:])
            if i < 4:
                nc.vector.tensor_copy(a_sb[t][:, BANK * h : BANK * (h + 1)], bank[:])
        for lo, hi in ((0, 384), (384, 512)):
            for t, bank in ((2, banks[7]), (3, banks[0])):
                nc.vector.tensor_copy(a_sb[t][:, BANK + lo : BANK + hi], bank[:, lo:hi])

        g4 = keep.tile([P, PACK, O], F32, name="g4")
        g5 = keep.tile([P, PACK, O], F32, name="g5")

        def fetch4(t, lo, hi):
            nc.scalar.activation(g4[:, t, lo:hi], a_sb[t][:].indirect(entries(list4, lo, hi)), COPY, scale=sa_sb[:, t : t + 1])

        def fetch5(t, lo, hi):
            nc.scalar.activation(g5[:, t, lo:hi], a_sb[t][:].indirect(entries(list5, lo, hi)), COPY, scale=sb_sb[:, t : t + 1])

        hid_in = keep.tile([P, O, PACK], BF16, name="hid_in", align_bytes=64)
        hid_w = keep.tile([P, O], U32, name="hid_w", align_bytes=64)
        hid_s = keep.tile([P, O], U8, name="hid_s", align_bytes=64)

        half_o = O // 2
        hid = keep.tile([P, PACK, half_o], BF16, name="hid")

        def larger(ts, lo, hi):
            cols = slice(lo % half_o, lo % half_o + hi - lo)
            nc.vector.tensor_tensor(hid[:, ts, cols], g4[:, ts, lo:hi], g5[:, ts, lo:hi], MAX)

        def interleave_hidden(lo, hi):
            cols = slice(lo % half_o, lo % half_o + hi - lo)
            nc.vector.tensor_copy(
                hid_in[:, lo:hi, :].rearrange("p (c i) t -> p c t i", i=4),
                hid[:, :, cols].rearrange("p t (c i) -> p c t i", i=4),
            )

        def quantize_hidden(lo, hi):
            nc.vector.quantize_mx(hid_w[:, lo:hi].bitcast(FP8X4), hid_s[:, lo:hi], hid_in[:, lo:hi, :].rearrange("p o t -> p (o t)"))

        def second_product(lo, hi, first_bank, copies_out):
            for b in range(N // P):
                acc = banks[first_bank + b][:, : hi - lo]
                nc.tensor.matmul_mx(acc, lhsT=wb_w[:, 2 * P * b : 2 * P * (b + 1)].bitcast(FP4X4), lhsT_scale=wb_s[:, P * b : P * (b + 1)],
                                    rhs=hid_w[:, lo:hi].bitcast(FP8X4), rhs_scale=hid_s[:, lo:hi], start=True, stop=True)
                copies_out[b](p_sb[b][:, lo:hi], acc)

        for t in range(2):
            fetch5(t, 0, O)
            fetch4(t, 0, O)
        for t, ts in ((2, slice(0, 3)), (3, slice(3, PACK))):
            fetch5(t, 0, half_o)
            fetch4(t, 0, half_o)
            larger(ts, 0, half_o)
        interleave_hidden(0, half_o)
        larger(slice(0, 2), half_o, O)
        quantize_hidden(0, half_o)
        for t in range(2, PACK):
            fetch5(t, half_o, O)
        for lo in range(half_o, O, 128):
            for t in range(2, PACK):
                fetch4(t, lo, lo + 128)
                larger(slice(t, t + 1), lo, lo + 128)
            interleave_hidden(lo, lo + 128)
            quantize_hidden(lo, lo + 128)
        p_sb = [keep.tile([P, O], F32, name="p%d" % b, tag="a%d" % (3 - b)) for b in range(N // P)]
        second_product(0, 256, 1, [nc.scalar.copy, nc.scalar.copy])
        second_product(256, 384, 3, [nc.scalar.copy, nc.scalar.copy])
        second_product(384, O, 5, [nc.scalar.copy, nc.vector.tensor_copy])

        m0 = keep.tile([P, N // P, U], F32, name="m0")
        for b, lo, hi in ((0, 0, U // 2), (1, 0, U), (0, U // 2, U)):
            nc.scalar.activation(m0[:, b, lo:hi], p_sb[b][:].indirect(entries(list6, lo, hi)), COPY, scale=so_sb[b][:])
            nc.vector.tensor_copy(pages[b][:].indirect(entries(list7, lo, hi)), m0[:, b, lo:hi])
            if hi == U:
                nc.sync.dma_start(out[b * P : (b + 1) * P, :], pages[b][:])
